import numpy as np
import ml_dtypes


def mxq(x, axis, fmt="e4m3"):
    dtype, down = {"e4m3": (ml_dtypes.float8_e4m3fn, 7), "e5m2": (ml_dtypes.float8_e5m2, 14)}[fmt]
    v = np.moveaxis(np.asarray(x, np.float32).astype(ml_dtypes.bfloat16).astype(np.float64), axis, -1)
    blocks = v.reshape(v.shape[:-1] + (-1, 32))
    amax = np.abs(blocks).max(-1, keepdims=True)
    byte = np.maximum(np.where(amax > 0, np.frexp(amax)[1] - 1 + 127, 0) - down, 1)
    scale = np.exp2(byte - 127.0)
    codes = (blocks / scale).astype(np.float32).astype(dtype).astype(np.float64)
    return np.moveaxis((codes * scale).reshape(v.shape), -1, axis)


WIDE = False


def mx_kscale(k):
    if not WIDE:
        return np.ones(k)
    levels = np.array([10, -10, 5, -5, 0])
    if k % 512:
        return np.exp2(np.random.permutation(np.resize(levels, k // 32))).repeat(32)
    a = np.empty((k // 512, 16))
    for p in range(k // 512):
        a[p, :8] = np.random.permutation(np.resize(levels, 8))
        for g in range(8):
            far = levels[np.abs(levels - a[p, g]) >= 10]
            a[p, g + 8] = far[np.random.randint(len(far))]
    return np.exp2(a.ravel()).repeat(32)


def f64(x):
    return np.asarray(x).astype(np.float64)


def striped(idx):
    return np.tile(idx.reshape(-1, 16).T, (8, 1)).astype(np.uint16)


def unstriped(offs):
    return offs[:16].T.reshape(-1).astype(np.int64)


def pack_weight(w):
    k, n = w.shape
    w = f64(np.asarray(w, np.float32).astype(ml_dtypes.bfloat16)).reshape(k // 32, 32, n)
    amax = np.abs(w).max(1)
    byte = np.clip(np.where(amax > 0, np.frexp(amax)[1] - 1 + 127 - 7, 1), 1, 254)
    scaled = (w * np.exp2(127.0 - byte)[:, None, :]).reshape(k, n).astype(np.float32)
    words = np.ascontiguousarray(scaled.reshape(k // 512, 128, 4, n).transpose(0, 1, 3, 2)).astype(ml_dtypes.float8_e4m3fn).view(np.uint8)
    return words, np.ascontiguousarray(byte.astype(np.uint8).reshape(k // 512, 16, n))


def unpack_weight(words, scales):
    g, p, n, _ = words.shape
    vals = np.ascontiguousarray(words).view(ml_dtypes.float8_e4m3fn).astype(np.float64) * np.repeat(np.exp2(scales.astype(np.float64) - 127.0), 8, axis=1)[..., None]
    return vals.transpose(0, 1, 3, 2).reshape(g * 512, n)


K, T, S, D, N, U = 512, 2048, 512, 8, 128, 1024
P = 2 ** 7


def setup_inputs():
    n = np.random.standard_normal
    s = mx_kscale(K)[:, None]
    packed_xT = pack_weight(n((K, T)) * s)
    return {
        "x_words": packed_xT[0],
        "x_scales": packed_xT[1],
        "w1": (n((K, N)) / np.sqrt(K) / s).astype(np.float32),
        "lr": (np.tile(0.3 * n(U), (P, 1))).astype(np.float32),
        "lo": (np.tile(np.random.uniform(0.75, 0.85, U), (P, 1))).astype(np.float32),
        "hi": (np.tile(np.random.uniform(1.15, 1.3, U), (P, 1))).astype(np.float32),
        "rf": (np.tile(0.3 * n(U), (P, 1))).astype(np.float32),
        "offs": striped(np.random.permutation(T)[:S]),
        "ans": striped(np.random.permutation(np.concatenate([np.arange(S), np.random.randint(0, S, U - S)]))),
    }


def reference(x_words, x_scales, w1, lr, lo, hi, rf, offs, ans):
    xq = unpack_weight(x_words, x_scales)[:, unstriped(offs)]
    y = mxq(f64(w1), 0, "e4m3").T @ xq
    my = y.reshape(len(y), -1, D).mean(axis=2)
    dd = y - np.repeat(my, D, axis=1)
    d2 = (dd) ** 2
    sd = np.sqrt(d2.reshape(len(d2), -1, D).mean(axis=2) + 0.1)
    adv = dd / np.repeat(sd, D, axis=1)
    at = adv[:, unstriped(ans)]
    ratio = np.exp(f64(lr)[:1])
    clip = np.minimum(np.maximum(ratio, f64(lo)[:1]), f64(hi)[:1])
    kl = 0.2 * (np.exp(f64(rf)[:1]) - f64(rf)[:1] - 1.0)
    return np.minimum(at * ratio, at * clip) - kl

@@ -1,0 +1,203 @@
+from contextlib import ExitStack
+
+import concourse.mybir as mybir
+from concourse.masks import make_identity
+
+K, T, S, D, M, U = 512, 2048, 512, 8, 128, 1024
+P = 128
+PACK = 4
+HALF = S // 2
+GROUPS = HALF // D
+BLOCKS = U // P
+CHUNK = 256
+TURNED_CHUNKS = 2
+TINY = 1e-30
+
+FLOPS = 2 * K * M * S
+BYTES = K * T + 16 * T + 4 * K * M + 4 * 4 * U + 2 * P * (S + U) // 16 + 4 * M * U
+
+F32 = mybir.dt.float32
+BF16 = mybir.dt.bfloat16
+I32 = mybir.dt.int32
+U32 = mybir.dt.uint32
+U16 = mybir.dt.uint16
+U8 = mybir.dt.uint8
+FP8X4 = mybir.dt.float8_e4m3fn_x4
+ALU = mybir.AluOpType
+ACT = mybir.ActivationFunctionType
+AXIS_X = mybir.AxisListType.X
+
+
+def tile_picked_ygrpo_kl_p_kernel(
+    tc, x_words, x_scales, w1, lr, lo, hi, rf, offs, ans, out
+):
+    nc = tc.nc
+    chunks = U // CHUNK
+    per_chunk = CHUNK // P
+    with ExitStack() as ctx:
+        sb = ctx.enter_context(tc.tile_pool(name="sb", bufs=1))
+        ps = ctx.enter_context(tc.psum_pool(name="ps", bufs=1))
+
+        offs_sb = sb.tile([P, S // 16], U16, name="offs_sb")
+        ans_sb = sb.tile([P, U // 16], U16, name="ans_sb")
+        table_words = sb.tile([P, T], U32, name="table_words", align_bytes=64)
+        table_scales = sb.tile([P, T], U8, name="table_scales", align_bytes=64)
+        w_raw = sb.tile([P, PACK, M], F32, name="w_raw")
+        rows = sb.tile([P, 2, P], F32, name="rows")
+        ident = sb.tile([P, P], F32, name="ident")
+
+        nc.gpsimd.memset(table_scales[:].bitcast(I32), 0)
+        make_identity(nc, ident[:])
+        nc.gpsimd.memset(rows[:], 0.0)
+
+        def as_rows(vec):
+            return vec[0:1, :].rearrange("o (b t) -> (o b) t", t=P)
+
+        nc.sync.dma_start(offs_sb[:], offs)
+        nc.sync.dma_start(w_raw[:], w1.rearrange("(p j) m -> p j m", j=PACK))
+        scale_rows = x_scales[0].bitcast(I32)
+        for q in range(4):
+            nc.sync.dma_start(table_scales[:].bitcast(I32)[32 * q : 32 * q + 4, :], scale_rows[4 * q : 4 * q + 4, :])
+        nc.sync.dma_start(table_words[:].bitcast(I32), x_words[0].rearrange("p n t -> p (n t)").bitcast(I32))
+        nc.scalar.dma_start(rows[0:8, 0, :], as_rows(lr))
+        nc.scalar.dma_start(rows[8:16, 0, :], as_rows(rf))
+        nc.sync.dma_start(rows[16:24, 0, :], as_rows(lo))
+        nc.sync.dma_start(rows[24:32, 0, :], as_rows(hi))
+        nc.sync.dma_start(ans_sb[:], ans)
+
+        w_grouped = sb.tile([P, M, PACK], BF16, name="w_grouped", align_bytes=64)
+        w_codes = sb.tile([P, M], U32, name="w_codes", align_bytes=64)
+        w_scales = sb.tile([P, M], U8, name="w_scales", align_bytes=64)
+        nc.scalar.copy(w_grouped[:], w_raw[:].rearrange("p j m -> p m j"))
+
+        picked_scales = sb.tile([P, S], U8, name="picked_scales", align_bytes=64)
+        nc.vector.tensor_copy(picked_scales[:], table_scales[:].indirect(offs_sb[:]))
+        nc.vector.quantize_mx(
+            out=w_codes[:].bitcast(FP8X4), scales=w_scales[:], in_=w_grouped[:].rearrange("p m j -> p (m j)")
+        )
+
+        nc.scalar.activation(rows[0:16, 1, :], rows[0:16, 0, :], ACT.Exp)
+
+        picked_words = [sb.tile([P, HALF], U32, name="picked_words%d" % h, align_bytes=64) for h in range(2)]
+        y = [ps.tile([P, GROUPS, D], F32, name="y%d" % h, tag="wide%d" % h) for h in range(2)]
+        for h in range(2):
+            nc.vector.tensor_copy(picked_words[h][:], table_words[:].indirect(offs_sb[:, 16 * h : 16 * (h + 1)]))
+            nc.tensor.matmul_mx(
+                out=y[h][:].rearrange("p g d -> p (g d)"),
+                lhsT=w_codes[:].bitcast(FP8X4),
+                lhsT_scale=w_scales[:],
+                rhs=picked_words[h][:].bitcast(FP8X4),
+                rhs_scale=picked_scales[:, h * HALF : (h + 1) * HALF],
+                start=True,
+                stop=True,
+            )
+
+        sums = [sb.tile([P, GROUPS], F32, name="sums%d" % h) for h in range(2)]
+        dev = [sb.tile([P, GROUPS, D], F32, name="dev%d" % h) for h in range(2)]
+        sq = [sb.tile([P, GROUPS, D], F32, name="sq%d" % h) for h in range(2)]
+        sq_sums = [sb.tile([P, GROUPS], F32, name="sq_sums%d" % h) for h in range(2)]
+        inv_sd = [sb.tile([P, GROUPS], F32, name="inv_sd%d" % h) for h in range(2)]
+        adv = sb.tile([P, S], F32, name="adv")
+
+        def over_group(t):
+            return t[:].unsqueeze(2).to_broadcast([P, GROUPS, D])
+
+        for h in range(2):
+            nc.vector.tensor_reduce(sums[h][:], y[h][:], AXIS_X, ALU.add)
+        for h in range(2):
+            nc.vector.scalar_tensor_tensor(dev[h][:], over_group(sums[h]), -1.0 / D, y[h][:], ALU.mult, ALU.add)
+            nc.scalar.activation(sq[h][:], dev[h][:], ACT.Square)
+        for h in range(2):
+            nc.vector.tensor_reduce(sq_sums[h][:], sq[h][:], AXIS_X, ALU.add)
+            nc.scalar.activation(inv_sd[h][:], sq_sums[h][:], ACT.Abs_reciprocal_sqrt, bias=0.1, scale=1.0 / D)
+        for h in range(2):
+            nc.vector.tensor_tensor(
+                adv[:, h * HALF : (h + 1) * HALF].rearrange("p (g d) -> p g d", d=D),
+                dev[h][:],
+                over_group(inv_sd[h]),
+                ALU.mult,
+            )
+
+        cols = ps.tile([P, 2, P], F32, name="cols", tag="turn0")
+        for i in range(2):
+            nc.tensor.transpose(cols[:, i, :], rows[:, i, :], ident[:])
+        neg = sb.tile([P, 2, 32], F32, name="neg")
+        nc.vector.tensor_scalar(neg[:], cols[:, :, 0:32], -1.0, None, ALU.mult)
+        n_rf, n_lo, n_hi = neg[:, 0, 8:16], neg[:, 0, 16:24], neg[:, 0, 24:32]
+        n_ratio, n_erf = neg[:, 1, 0:8], neg[:, 1, 8:16]
+        n_min = sb.tile([P, BLOCKS], F32, name="n_min")
+        n_edge = sb.tile([P, BLOCKS], F32, name="n_edge")
+        n_max = sb.tile([P, BLOCKS], F32, name="n_max")
+        n_gap = sb.tile([P, BLOCKS], F32, name="n_gap")
+        inv_max = sb.tile([P, BLOCKS], F32, name="inv_max")
+        rho = sb.tile([P, BLOCKS], F32, name="rho")
+        kl5 = sb.tile([P, BLOCKS], F32, name="kl5")
+        kl = sb.tile([P, BLOCKS], F32, name="kl")
+        nc.vector.tensor_tensor(n_edge[:], n_lo, n_hi, ALU.max)
+        nc.vector.tensor_tensor(n_min[:], n_ratio, n_hi, ALU.max)
+        nc.vector.scalar_tensor_tensor(kl5[:], n_rf, -1.0, n_erf, ALU.add, ALU.subtract)
+        nc.vector.scalar_tensor_tensor(n_max[:], n_ratio, -TINY, n_edge[:], ALU.min, ALU.min)
+        nc.vector.tensor_scalar(kl[:], kl5[:], 0.2, None, ALU.mult)
+        nc.vector.reciprocal(inv_max[:], n_max[:])
+        nc.vector.tensor_tensor(n_gap[:], n_max[:], n_min[:], ALU.subtract)
+        nc.vector.tensor_tensor(rho[:], n_min[:], inv_max[:], ALU.mult)
+
+        first_direct = TURNED_CHUNKS * per_chunk
+        n_direct = BLOCKS - first_direct
+
+        def spread(col, name):
+            bank = ps.tile([P, n_direct * P], F32, name=name)
+            for j in range(n_direct):
+                b = first_direct + j
+                nc.tensor.transpose(bank[:, j * P : (j + 1) * P], col[:, b : b + 1].to_broadcast([P, P]), ident[:])
+            return bank
+
+        max_bank = spread(n_max, "max_bank")
+        n_max_wide = sb.tile([P, n_direct * P], F32, name="n_max_wide")
+        nc.scalar.copy(n_max_wide[:], max_bank[:])
+        rho_wide = spread(rho, "rho_wide")
+        kl_wide = spread(kl, "kl_wide")
+
+        got = [sb.tile([P, CHUNK], F32, name="got%d" % c) for c in range(chunks)]
+        res = [sb.tile([P, CHUNK], F32, name="res%d" % c) for c in range(chunks)]
+
+        def offsets(c):
+            return ans_sb[:, c * (CHUNK // 16) : (c + 1) * (CHUNK // 16)]
+
+        for c in range(TURNED_CHUNKS):
+            nc.vector.tensor_copy(got[c][:], adv[:].indirect(offsets(c)))
+        for c in range(TURNED_CHUNKS, chunks):
+            d0 = (c - TURNED_CHUNKS) * CHUNK
+            nc.vector.tensor_tensor(got[c][:], adv[:].indirect(offsets(c)), n_max_wide[:, d0 : d0 + CHUNK], ALU.mult)
+
+        back = []
+        for c in range(TURNED_CHUNKS):
+            turned = ps.tile([P, per_chunk, P], F32, name="turned%d" % c, tag="turn%d" % (1 - c % 2))
+            for j in range(per_chunk):
+                nc.tensor.transpose(turned[:, j, :], got[c][:, j * P : (j + 1) * P], ident[:])
+            bent = sb.tile([P, per_chunk, P], F32, name="bent%d" % c)
+            line = sb.tile([P, per_chunk, P], F32, name="line%d" % c)
+            bank = ps.tile([P, CHUNK], F32, name="back%d" % c, tag="wide%d" % (c % 2))
+            for j in range(per_chunk):
+                b = c * per_chunk + j
+                nc.scalar.activation(bent[:, j, :], turned[:, j, :], ACT.Relu, scale=n_gap[:, b : b + 1])
+                nc.scalar.activation(
+                    line[:, j, :], turned[:, j, :], ACT.Identity, scale=n_min[:, b : b + 1], bias=kl[:, b : b + 1]
+                )
+                cols_j = bank[:, j * P : (j + 1) * P]
+                nc.tensor.matmul(cols_j, bent[:, j, :], ident[:], start=True, stop=False, is_transpose=True)
+                nc.tensor.matmul(cols_j, line[:, j, :], ident[:], start=False, stop=True, is_transpose=True)
+            back.append(bank)
+
+        low = {c: sb.tile([P, CHUNK], F32, name="low%d" % c) for c in range(TURNED_CHUNKS, chunks)}
+        high = {c: sb.tile([P, CHUNK], F32, name="high%d" % c) for c in range(TURNED_CHUNKS, chunks)}
+        for c in range(TURNED_CHUNKS, chunks):
+            d0 = (c - TURNED_CHUNKS) * CHUNK
+            nc.vector.scalar_tensor_tensor(low[c][:], got[c][:], 0.0, rho_wide[:, d0 : d0 + CHUNK], ALU.min, ALU.mult)
+            nc.vector.scalar_tensor_tensor(high[c][:], got[c][:], 0.0, kl_wide[:, d0 : d0 + CHUNK], ALU.max, ALU.add)
+        for c in range(TURNED_CHUNKS):
+            nc.scalar.activation(res[c][:], back[c][:], ACT.Copy, scale=-1.0)
+            nc.sync.dma_start(out[:, c * CHUNK : (c + 1) * CHUNK], res[c][:])
+        for c in range(TURNED_CHUNKS, chunks):
+            nc.vector.scalar_tensor_tensor(res[c][:], low[c][:], -1.0, high[c][:], ALU.mult, ALU.subtract)
+            nc.sync.dma_start(out[:, c * CHUNK : (c + 1) * CHUNK], res[c][:])

@@ -7,10 +7,12 @@ K, T, S, D, M, U = 512, 2048, 512, 8, 128, 1024
 P = 128
 PACK = 4
 HALF = S // 2
-GROUPS = HALF // D
+PARTS = 4
+PART = S // PARTS
+GROUPS = PART // D
 BLOCKS = U // P
-CHUNK = 256
-TURNED_CHUNKS = 2
+TURNED = [1, 2, 2]
+DIRECT = [2, 1]
 TINY = 1e-30
 
 FLOPS = 2 * K * M * S
@@ -32,8 +34,6 @@ def tile_picked_ygrpo_kl_p_kernel(
     tc, x_words, x_scales, w1, lr, lo, hi, rf, offs, ans, out
 ):
     nc = tc.nc
-    chunks = U // CHUNK
-    per_chunk = CHUNK // P
     with ExitStack() as ctx:
         sb = ctx.enter_context(tc.tile_pool(name="sb", bufs=1))
         ps = ctx.enter_context(tc.psum_pool(name="ps", bufs=1))
@@ -47,8 +47,7 @@ def tile_picked_ygrpo_kl_p_kernel(
         ident = sb.tile([P, P], F32, name="ident")
 
         nc.gpsimd.memset(table_scales[:].bitcast(I32), 0)
-        make_identity(nc, ident[:])
-        nc.gpsimd.memset(rows[:], 0.0)
+        nc.vector.memset(rows[:], 0.0)
 
         def as_rows(vec):
             return vec[0:1, :].rearrange("o (b t) -> (o b) t", t=P)
@@ -58,9 +57,10 @@ def tile_picked_ygrpo_kl_p_kernel(
         scale_rows = x_scales[0].bitcast(I32)
         for q in range(4):
             nc.sync.dma_start(table_scales[:].bitcast(I32)[32 * q : 32 * q + 4, :], scale_rows[4 * q : 4 * q + 4, :])
+        nc.sync.dma_start(rows[0:8, 0, :], as_rows(lr))
+        nc.gpsimd.dma_start(rows[8:16, 0, :], as_rows(rf))
+        make_identity(nc, ident[:])
         nc.sync.dma_start(table_words[:].bitcast(I32), x_words[0].rearrange("p n t -> p (n t)").bitcast(I32))
-        nc.scalar.dma_start(rows[0:8, 0, :], as_rows(lr))
-        nc.scalar.dma_start(rows[8:16, 0, :], as_rows(rf))
         nc.sync.dma_start(rows[16:24, 0, :], as_rows(lo))
         nc.sync.dma_start(rows[24:32, 0, :], as_rows(hi))
         nc.sync.dma_start(ans_sb[:], ans)
@@ -77,109 +77,126 @@ def tile_picked_ygrpo_kl_p_kernel(
         )
 
         nc.scalar.activation(rows[0:16, 1, :], rows[0:16, 0, :], ACT.Exp)
+        warm = sb.tile([P, 1], F32, name="warm")
+        nc.scalar.activation(warm[0:16, :], rows[0:16, 1, 0:1], ACT.Abs_reciprocal_sqrt)
 
         picked_words = [sb.tile([P, HALF], U32, name="picked_words%d" % h, align_bytes=64) for h in range(2)]
-        y = [ps.tile([P, GROUPS, D], F32, name="y%d" % h, tag="wide%d" % h) for h in range(2)]
+        y = [ps.tile([P, GROUPS, D], F32, name="y%d" % i, tag="wide%d" % i) for i in range(PARTS)]
+        per_half = PARTS // 2
         for h in range(2):
             nc.vector.tensor_copy(picked_words[h][:], table_words[:].indirect(offs_sb[:, 16 * h : 16 * (h + 1)]))
-            nc.tensor.matmul_mx(
-                out=y[h][:].rearrange("p g d -> p (g d)"),
-                lhsT=w_codes[:].bitcast(FP8X4),
-                lhsT_scale=w_scales[:],
-                rhs=picked_words[h][:].bitcast(FP8X4),
-                rhs_scale=picked_scales[:, h * HALF : (h + 1) * HALF],
-                start=True,
-                stop=True,
-            )
-
-        sums = [sb.tile([P, GROUPS], F32, name="sums%d" % h) for h in range(2)]
-        dev = [sb.tile([P, GROUPS, D], F32, name="dev%d" % h) for h in range(2)]
-        sq = [sb.tile([P, GROUPS, D], F32, name="sq%d" % h) for h in range(2)]
-        sq_sums = [sb.tile([P, GROUPS], F32, name="sq_sums%d" % h) for h in range(2)]
-        inv_sd = [sb.tile([P, GROUPS], F32, name="inv_sd%d" % h) for h in range(2)]
-        adv = sb.tile([P, S], F32, name="adv")
-
-        def over_group(t):
-            return t[:].unsqueeze(2).to_broadcast([P, GROUPS, D])
-
-        for h in range(2):
-            nc.vector.tensor_reduce(sums[h][:], y[h][:], AXIS_X, ALU.add)
-        for h in range(2):
-            nc.vector.scalar_tensor_tensor(dev[h][:], over_group(sums[h]), -1.0 / D, y[h][:], ALU.mult, ALU.add)
-            nc.scalar.activation(sq[h][:], dev[h][:], ACT.Square)
-        for h in range(2):
-            nc.vector.tensor_reduce(sq_sums[h][:], sq[h][:], AXIS_X, ALU.add)
-            nc.scalar.activation(inv_sd[h][:], sq_sums[h][:], ACT.Abs_reciprocal_sqrt, bias=0.1, scale=1.0 / D)
-        for h in range(2):
-            nc.vector.tensor_tensor(
-                adv[:, h * HALF : (h + 1) * HALF].rearrange("p (g d) -> p g d", d=D),
-                dev[h][:],
-                over_group(inv_sd[h]),
-                ALU.mult,
-            )
+            for j in range(per_half):
+                i = h * per_half + j
+                nc.tensor.matmul_mx(
+                    out=y[i][:].rearrange("p g d -> p (g d)"),
+                    lhsT=w_codes[:].bitcast(FP8X4),
+                    lhsT_scale=w_scales[:],
+                    rhs=picked_words[h][:, j * PART : (j + 1) * PART].bitcast(FP8X4),
+                    rhs_scale=picked_scales[:, i * PART : (i + 1) * PART],
+                    start=True,
+                    stop=True,
+                )
 
         cols = ps.tile([P, 2, P], F32, name="cols", tag="turn0")
         for i in range(2):
             nc.tensor.transpose(cols[:, i, :], rows[:, i, :], ident[:])
         neg = sb.tile([P, 2, 32], F32, name="neg")
         nc.vector.tensor_scalar(neg[:], cols[:, :, 0:32], -1.0, None, ALU.mult)
-        n_rf, n_lo, n_hi = neg[:, 0, 8:16], neg[:, 0, 16:24], neg[:, 0, 24:32]
+        n_rf, n_hi = neg[:, 0, 8:16], neg[:, 0, 24:32]
         n_ratio, n_erf = neg[:, 1, 0:8], neg[:, 1, 8:16]
-        n_min = sb.tile([P, BLOCKS], F32, name="n_min")
-        n_edge = sb.tile([P, BLOCKS], F32, name="n_edge")
+        n_lo_ratio = neg[:].rearrange("p a (b c) -> p (a b) c", c=BLOCKS)[:, 2:5:2, :]
+        below_hi = sb.tile([P, 2, BLOCKS], F32, name="below_hi")
+        n_edge, n_min = below_hi[:, 0, :], below_hi[:, 1, :]
         n_max = sb.tile([P, BLOCKS], F32, name="n_max")
         n_gap = sb.tile([P, BLOCKS], F32, name="n_gap")
         inv_max = sb.tile([P, BLOCKS], F32, name="inv_max")
-        rho = sb.tile([P, BLOCKS], F32, name="rho")
+        n_rho = sb.tile([P, BLOCKS], F32, name="n_rho")
         kl5 = sb.tile([P, BLOCKS], F32, name="kl5")
         kl = sb.tile([P, BLOCKS], F32, name="kl")
-        nc.vector.tensor_tensor(n_edge[:], n_lo, n_hi, ALU.max)
-        nc.vector.tensor_tensor(n_min[:], n_ratio, n_hi, ALU.max)
+        nc.vector.tensor_tensor(below_hi[:], n_lo_ratio, n_hi.unsqueeze(1).to_broadcast([P, 2, BLOCKS]), ALU.max)
         nc.vector.scalar_tensor_tensor(kl5[:], n_rf, -1.0, n_erf, ALU.add, ALU.subtract)
-        nc.vector.scalar_tensor_tensor(n_max[:], n_ratio, -TINY, n_edge[:], ALU.min, ALU.min)
-        nc.vector.tensor_scalar(kl[:], kl5[:], 0.2, None, ALU.mult)
+        nc.vector.scalar_tensor_tensor(n_max[:], n_ratio, -TINY, n_edge, ALU.min, ALU.min)
+        nc.scalar.activation(kl[:], kl5[:], ACT.Copy, scale=0.2)
         nc.vector.reciprocal(inv_max[:], n_max[:])
-        nc.vector.tensor_tensor(n_gap[:], n_max[:], n_min[:], ALU.subtract)
-        nc.vector.tensor_tensor(rho[:], n_min[:], inv_max[:], ALU.mult)
+        nc.vector.tensor_tensor(n_gap[:], n_max[:], n_min, ALU.subtract)
+        nc.vector.scalar_tensor_tensor(n_rho[:], n_min, -1.0, inv_max[:], ALU.mult, ALU.mult)
 
-        first_direct = TURNED_CHUNKS * per_chunk
-        n_direct = BLOCKS - first_direct
+        first_direct = sum(TURNED)
+        n_direct = sum(DIRECT)
 
-        def spread(col, name):
-            bank = ps.tile([P, n_direct * P], F32, name=name)
+        def spread(col, name, tag):
+            bank = ps.tile([P, n_direct * P], F32, name=name, tag=tag)
             for j in range(n_direct):
                 b = first_direct + j
                 nc.tensor.transpose(bank[:, j * P : (j + 1) * P], col[:, b : b + 1].to_broadcast([P, P]), ident[:])
             return bank
 
-        max_bank = spread(n_max, "max_bank")
+        max_bank = spread(n_max, "max_bank", "turn1")
         n_max_wide = sb.tile([P, n_direct * P], F32, name="n_max_wide")
         nc.scalar.copy(n_max_wide[:], max_bank[:])
-        rho_wide = spread(rho, "rho_wide")
-        kl_wide = spread(kl, "kl_wide")
+        rho_wide = spread(n_rho, "rho_wide", "rho")
+        kl_wide = spread(kl, "kl_wide", "kl")
 
-        got = [sb.tile([P, CHUNK], F32, name="got%d" % c) for c in range(chunks)]
-        res = [sb.tile([P, CHUNK], F32, name="res%d" % c) for c in range(chunks)]
+        sums = [sb.tile([P, GROUPS], F32, name="sums%d" % i) for i in range(PARTS)]
+        dev = [sb.tile([P, GROUPS, D], F32, name="dev%d" % i) for i in range(PARTS)]
+        sq = [sb.tile([P, GROUPS, D], F32, name="sq%d" % i) for i in range(PARTS)]
+        sq_sums = [sb.tile([P, GROUPS], F32, name="sq_sums%d" % i) for i in range(PARTS)]
+        inv_sd = [sb.tile([P, GROUPS], F32, name="inv_sd%d" % i) for i in range(PARTS)]
+        adv = sb.tile([P, S], F32, name="adv")
+
+        def over_group(t):
+            return t[:].unsqueeze(2).to_broadcast([P, GROUPS, D])
+
+        for h in range(2):
+            mine = range(h * per_half, (h + 1) * per_half)
+            for i in mine:
+                nc.vector.tensor_reduce(sums[i][:], y[i][:], AXIS_X, ALU.add)
+            for i in mine:
+                nc.vector.scalar_tensor_tensor(dev[i][:], over_group(sums[i]), -1.0 / D, y[i][:], ALU.mult, ALU.add)
+                nc.scalar.activation(sq[i][:], dev[i][:], ACT.Square)
+        for i in range(PARTS):
+            nc.vector.tensor_reduce(sq_sums[i][:], sq[i][:], AXIS_X, ALU.add)
+            nc.scalar.activation(inv_sd[i][:], sq_sums[i][:], ACT.Abs_reciprocal_sqrt, bias=0.1, scale=1.0 / D)
+        for i in range(PARTS):
+            nc.vector.tensor_tensor(
+                adv[:, i * PART : (i + 1) * PART].rearrange("p (g d) -> p g d", d=D),
+                dev[i][:],
+                over_group(inv_sd[i]),
+                ALU.mult,
+            )
+
+        widths = TURNED + DIRECT
+        starts = [sum(widths[:c]) for c in range(len(widths))]
+        got = [sb.tile([P, n * P], F32, name="got%d" % c) for c, n in enumerate(widths)]
+        res = [sb.tile([P, n * P], F32, name="res%d" % c) for c, n in enumerate(widths)]
+        turned_chunks = range(len(TURNED))
+        direct_chunks = range(len(TURNED), len(widths))
 
         def offsets(c):
-            return ans_sb[:, c * (CHUNK // 16) : (c + 1) * (CHUNK // 16)]
+            return ans_sb[:, starts[c] * 8 : (starts[c] + widths[c]) * 8]
 
-        for c in range(TURNED_CHUNKS):
+        def tokens(c):
+            return slice(starts[c] * P, (starts[c] + widths[c]) * P)
+
+        def wide_cols(c):
+            return slice((starts[c] - first_direct) * P, (starts[c] - first_direct + widths[c]) * P)
+
+        for c in turned_chunks:
             nc.vector.tensor_copy(got[c][:], adv[:].indirect(offsets(c)))
-        for c in range(TURNED_CHUNKS, chunks):
-            d0 = (c - TURNED_CHUNKS) * CHUNK
-            nc.vector.tensor_tensor(got[c][:], adv[:].indirect(offsets(c)), n_max_wide[:, d0 : d0 + CHUNK], ALU.mult)
+        for c in direct_chunks:
+            nc.vector.tensor_tensor(got[c][:], adv[:].indirect(offsets(c)), n_max_wide[:, wide_cols(c)], ALU.mult)
 
         back = []
-        for c in range(TURNED_CHUNKS):
-            turned = ps.tile([P, per_chunk, P], F32, name="turned%d" % c, tag="turn%d" % (1 - c % 2))
-            for j in range(per_chunk):
+        for c in turned_chunks:
+            n = widths[c]
+            turned = ps.tile([P, n, P], F32, name="turned%d" % c, tag=["turn0", "turn1", "wide3"][c])
+            for j in range(n):
                 nc.tensor.transpose(turned[:, j, :], got[c][:, j * P : (j + 1) * P], ident[:])
-            bent = sb.tile([P, per_chunk, P], F32, name="bent%d" % c)
-            line = sb.tile([P, per_chunk, P], F32, name="line%d" % c)
-            bank = ps.tile([P, CHUNK], F32, name="back%d" % c, tag="wide%d" % (c % 2))
-            for j in range(per_chunk):
-                b = c * per_chunk + j
+            bent = sb.tile([P, n, P], F32, name="bent%d" % c)
+            line = sb.tile([P, n, P], F32, name="line%d" % c)
+            bank = ps.tile([P, n * P], F32, name="back%d" % c, tag=["wide0", "wide1", "wide2"][c])
+            for j in range(n):
+                b = starts[c] + j
                 nc.scalar.activation(bent[:, j, :], turned[:, j, :], ACT.Relu, scale=n_gap[:, b : b + 1])
                 nc.scalar.activation(
                     line[:, j, :], turned[:, j, :], ACT.Identity, scale=n_min[:, b : b + 1], bias=kl[:, b : b + 1]
@@ -189,15 +206,14 @@ def tile_picked_ygrpo_kl_p_kernel(
                 nc.tensor.matmul(cols_j, line[:, j, :], ident[:], start=False, stop=True, is_transpose=True)
             back.append(bank)
 
-        low = {c: sb.tile([P, CHUNK], F32, name="low%d" % c) for c in range(TURNED_CHUNKS, chunks)}
-        high = {c: sb.tile([P, CHUNK], F32, name="high%d" % c) for c in range(TURNED_CHUNKS, chunks)}
-        for c in range(TURNED_CHUNKS, chunks):
-            d0 = (c - TURNED_CHUNKS) * CHUNK
-            nc.vector.scalar_tensor_tensor(low[c][:], got[c][:], 0.0, rho_wide[:, d0 : d0 + CHUNK], ALU.min, ALU.mult)
-            nc.vector.scalar_tensor_tensor(high[c][:], got[c][:], 0.0, kl_wide[:, d0 : d0 + CHUNK], ALU.max, ALU.add)
-        for c in range(TURNED_CHUNKS):
+        low = {c: sb.tile([P, widths[c] * P], F32, name="low%d" % c) for c in direct_chunks}
+        high = {c: sb.tile([P, widths[c] * P], F32, name="high%d" % c) for c in direct_chunks}
+        for c in direct_chunks:
+            nc.vector.scalar_tensor_tensor(low[c][:], got[c][:], 0.0, rho_wide[:, wide_cols(c)], ALU.min, ALU.mult)
+            nc.vector.scalar_tensor_tensor(high[c][:], got[c][:], 0.0, kl_wide[:, wide_cols(c)], ALU.max, ALU.add)
+        for c in turned_chunks:
             nc.scalar.activation(res[c][:], back[c][:], ACT.Copy, scale=-1.0)
-            nc.sync.dma_start(out[:, c * CHUNK : (c + 1) * CHUNK], res[c][:])
-        for c in range(TURNED_CHUNKS, chunks):
-            nc.vector.scalar_tensor_tensor(res[c][:], low[c][:], -1.0, high[c][:], ALU.mult, ALU.subtract)
-            nc.sync.dma_start(out[:, c * CHUNK : (c + 1) * CHUNK], res[c][:])
+            nc.sync.dma_start(out[:, tokens(c)], res[c][:])
+        for c in direct_chunks:
+            nc.vector.tensor_tensor(res[c][:], low[c][:], high[c][:], ALU.subtract)
+            nc.sync.dma_start(out[:, tokens(c)], res[c][:])

@@ -101,7 +101,7 @@ def tile_picked_ygrpo_kl_p_kernel(
         for i in range(2):
             nc.tensor.transpose(cols[:, i, :], rows[:, i, :], ident[:])
         neg = sb.tile([P, 2, 32], F32, name="neg")
-        nc.vector.tensor_scalar(neg[:], cols[:, :, 0:32], -1.0, None, ALU.mult)
+        nc.scalar.activation(neg[:], cols[:, :, 0:32], ACT.Copy, scale=-1.0)
         n_rf, n_hi = neg[:, 0, 8:16], neg[:, 0, 24:32]
         n_ratio, n_erf = neg[:, 1, 0:8], neg[:, 1, 8:16]
         n_lo_ratio = neg[:].rearrange("p a (b c) -> p (a b) c", c=BLOCKS)[:, 2:5:2, :]
@@ -110,16 +110,16 @@ def tile_picked_ygrpo_kl_p_kernel(
         n_max = sb.tile([P, BLOCKS], F32, name="n_max")
         n_gap = sb.tile([P, BLOCKS], F32, name="n_gap")
         inv_max = sb.tile([P, BLOCKS], F32, name="inv_max")
-        n_rho = sb.tile([P, BLOCKS], F32, name="n_rho")
+        rho = sb.tile([P, BLOCKS], F32, name="rho")
         kl5 = sb.tile([P, BLOCKS], F32, name="kl5")
         kl = sb.tile([P, BLOCKS], F32, name="kl")
         nc.vector.tensor_tensor(below_hi[:], n_lo_ratio, n_hi.unsqueeze(1).to_broadcast([P, 2, BLOCKS]), ALU.max)
-        nc.vector.scalar_tensor_tensor(kl5[:], n_rf, -1.0, n_erf, ALU.add, ALU.subtract)
+        nc.gpsimd.tensor_tensor(kl5[:], n_rf, n_erf, ALU.subtract)
         nc.vector.scalar_tensor_tensor(n_max[:], n_ratio, -TINY, n_edge, ALU.min, ALU.min)
-        nc.scalar.activation(kl[:], kl5[:], ACT.Copy, scale=0.2)
+        nc.scalar.activation(kl[:], kl5[:], ACT.Copy, scale=0.2, bias=-0.2)
         nc.vector.reciprocal(inv_max[:], n_max[:])
-        nc.vector.tensor_tensor(n_gap[:], n_max[:], n_min, ALU.subtract)
-        nc.vector.scalar_tensor_tensor(n_rho[:], n_min, -1.0, inv_max[:], ALU.mult, ALU.mult)
+        nc.gpsimd.tensor_tensor(n_gap[:], n_max[:], n_min, ALU.subtract)
+        nc.gpsimd.tensor_tensor(rho[:], n_min, inv_max[:], ALU.mult)
 
         first_direct = sum(TURNED)
         n_direct = sum(DIRECT)
@@ -134,7 +134,7 @@ def tile_picked_ygrpo_kl_p_kernel(
         max_bank = spread(n_max, "max_bank", "turn1")
         n_max_wide = sb.tile([P, n_direct * P], F32, name="n_max_wide")
         nc.scalar.copy(n_max_wide[:], max_bank[:])
-        rho_wide = spread(n_rho, "rho_wide", "rho")
+        rho_wide = spread(rho, "rho_wide", "rho")
         kl_wide = spread(kl, "kl_wide", "kl")
 
         sums = [sb.tile([P, GROUPS], F32, name="sums%d" % i) for i in range(PARTS)]
@@ -213,7 +213,8 @@ def tile_picked_ygrpo_kl_p_kernel(
             nc.vector.scalar_tensor_tensor(high[c][:], got[c][:], 0.0, kl_wide[:, wide_cols(c)], ALU.max, ALU.add)
         for c in turned_chunks:
             nc.scalar.activation(res[c][:], back[c][:], ACT.Copy, scale=-1.0)
-            nc.sync.dma_start(out[:, tokens(c)], res[c][:])
+            queue = nc.scalar if c == turned_chunks[-1] else nc.sync
+            queue.dma_start(out[:, tokens(c)], res[c][:])
         for c in direct_chunks:
-            nc.vector.tensor_tensor(res[c][:], low[c][:], high[c][:], ALU.subtract)
+            nc.vector.scalar_tensor_tensor(res[c][:], low[c][:], -1.0, high[c][:], ALU.mult, ALU.subtract)
             nc.sync.dma_start(out[:, tokens(c)], res[c][:])

from contextlib import ExitStack

import concourse.mybir as mybir
from concourse.masks import make_identity

K, T, S, D, M, U = 512, 2048, 512, 8, 128, 1024
P = 128
PACK = 4
HALF = S // 2
PARTS = 4
PART = S // PARTS
GROUPS = PART // D
BLOCKS = U // P
TURNED = [1, 2, 2]
DIRECT = [2, 1]
TINY = 1e-30

FLOPS = 2 * K * M * S
BYTES = K * T + 16 * T + 4 * K * M + 4 * 4 * U + 2 * P * (S + U) // 16 + 4 * M * U

F32 = mybir.dt.float32
BF16 = mybir.dt.bfloat16
I32 = mybir.dt.int32
U32 = mybir.dt.uint32
U16 = mybir.dt.uint16
U8 = mybir.dt.uint8
FP8X4 = mybir.dt.float8_e4m3fn_x4
ALU = mybir.AluOpType
ACT = mybir.ActivationFunctionType
AXIS_X = mybir.AxisListType.X


def tile_picked_ygrpo_kl_p_kernel(
    tc, x_words, x_scales, w1, lr, lo, hi, rf, offs, ans, out
):
    nc = tc.nc
    with ExitStack() as ctx:
        sb = ctx.enter_context(tc.tile_pool(name="sb", bufs=1))
        ps = ctx.enter_context(tc.psum_pool(name="ps", bufs=1))

        offs_sb = sb.tile([P, S // 16], U16, name="offs_sb")
        ans_sb = sb.tile([P, U // 16], U16, name="ans_sb")
        table_words = sb.tile([P, T], U32, name="table_words", align_bytes=64)
        table_scales = sb.tile([P, T], U8, name="table_scales", align_bytes=64)
        w_raw = sb.tile([P, PACK, M], F32, name="w_raw")
        rows = sb.tile([P, 2, P], F32, name="rows")
        ident = sb.tile([P, P], F32, name="ident")

        nc.gpsimd.memset(table_scales[:].bitcast(I32), 0)
        nc.vector.memset(rows[:], 0.0)

        def as_rows(vec):
            return vec[0:1, :].rearrange("o (b t) -> (o b) t", t=P)

        nc.sync.dma_start(offs_sb[:], offs)
        nc.sync.dma_start(w_raw[:], w1.rearrange("(p j) m -> p j m", j=PACK))
        scale_rows = x_scales[0].bitcast(I32)
        for q in range(4):
            nc.sync.dma_start(table_scales[:].bitcast(I32)[32 * q : 32 * q + 4, :], scale_rows[4 * q : 4 * q + 4, :])
        nc.sync.dma_start(rows[0:8, 0, :], as_rows(lr))
        nc.gpsimd.dma_start(rows[8:16, 0, :], as_rows(rf))
        make_identity(nc, ident[:])
        nc.sync.dma_start(table_words[:].bitcast(I32), x_words[0].rearrange("p n t -> p (n t)").bitcast(I32))
        nc.sync.dma_start(rows[16:24, 0, :], as_rows(lo))
        nc.sync.dma_start(rows[24:32, 0, :], as_rows(hi))
        nc.sync.dma_start(ans_sb[:], ans)

        w_grouped = sb.tile([P, M, PACK], BF16, name="w_grouped", align_bytes=64)
        w_codes = sb.tile([P, M], U32, name="w_codes", align_bytes=64)
        w_scales = sb.tile([P, M], U8, name="w_scales", align_bytes=64)
        nc.scalar.copy(w_grouped[:], w_raw[:].rearrange("p j m -> p m j"))

        picked_scales = sb.tile([P, S], U8, name="picked_scales", align_bytes=64)
        nc.vector.tensor_copy(picked_scales[:], table_scales[:].indirect(offs_sb[:]))
        nc.vector.quantize_mx(
            out=w_codes[:].bitcast(FP8X4), scales=w_scales[:], in_=w_grouped[:].rearrange("p m j -> p (m j)")
        )

        nc.scalar.activation(rows[0:16, 1, :], rows[0:16, 0, :], ACT.Exp)
        warm = sb.tile([P, 1], F32, name="warm")
        nc.scalar.activation(warm[0:16, :], rows[0:16, 1, 0:1], ACT.Abs_reciprocal_sqrt)

        picked_words = [sb.tile([P, HALF], U32, name="picked_words%d" % h, align_bytes=64) for h in range(2)]
        y = [ps.tile([P, GROUPS, D], F32, name="y%d" % i, tag="wide%d" % i) for i in range(PARTS)]
        per_half = PARTS // 2
        for h in range(2):
            nc.vector.tensor_copy(picked_words[h][:], table_words[:].indirect(offs_sb[:, 16 * h : 16 * (h + 1)]))
            for j in range(per_half):
                i = h * per_half + j
                nc.tensor.matmul_mx(
                    out=y[i][:].rearrange("p g d -> p (g d)"),
                    lhsT=w_codes[:].bitcast(FP8X4),
                    lhsT_scale=w_scales[:],
                    rhs=picked_words[h][:, j * PART : (j + 1) * PART].bitcast(FP8X4),
                    rhs_scale=picked_scales[:, i * PART : (i + 1) * PART],
                    start=True,
                    stop=True,
                )

        cols = ps.tile([P, 2, P], F32, name="cols", tag="turn0")
        for i in range(2):
            nc.tensor.transpose(cols[:, i, :], rows[:, i, :], ident[:])
        neg = sb.tile([P, 2, 32], F32, name="neg")
        nc.scalar.activation(neg[:], cols[:, :, 0:32], ACT.Copy, scale=-1.0)
        n_rf, n_hi = neg[:, 0, 8:16], neg[:, 0, 24:32]
        n_ratio, n_erf = neg[:, 1, 0:8], neg[:, 1, 8:16]
        n_lo_ratio = neg[:].rearrange("p a (b c) -> p (a b) c", c=BLOCKS)[:, 2:5:2, :]
        below_hi = sb.tile([P, 2, BLOCKS], F32, name="below_hi")
        n_edge, n_min = below_hi[:, 0, :], below_hi[:, 1, :]
        n_max = sb.tile([P, BLOCKS], F32, name="n_max")
        n_gap = sb.tile([P, BLOCKS], F32, name="n_gap")
        inv_max = sb.tile([P, BLOCKS], F32, name="inv_max")
        rho = sb.tile([P, BLOCKS], F32, name="rho")
        kl5 = sb.tile([P, BLOCKS], F32, name="kl5")
        kl = sb.tile([P, BLOCKS], F32, name="kl")
        nc.vector.tensor_tensor(below_hi[:], n_lo_ratio, n_hi.unsqueeze(1).to_broadcast([P, 2, BLOCKS]), ALU.max)
        nc.gpsimd.tensor_tensor(kl5[:], n_rf, n_erf, ALU.subtract)
        nc.vector.scalar_tensor_tensor(n_max[:], n_ratio, -TINY, n_edge, ALU.min, ALU.min)
        nc.scalar.activation(kl[:], kl5[:], ACT.Copy, scale=0.2, bias=-0.2)
        nc.vector.reciprocal(inv_max[:], n_max[:])
        nc.gpsimd.tensor_tensor(n_gap[:], n_max[:], n_min, ALU.subtract)
        nc.gpsimd.tensor_tensor(rho[:], n_min, inv_max[:], ALU.mult)

        first_direct = sum(TURNED)
        n_direct = sum(DIRECT)

        def spread(col, name, tag):
            bank = ps.tile([P, n_direct * P], F32, name=name, tag=tag)
            for j in range(n_direct):
                b = first_direct + j
                nc.tensor.transpose(bank[:, j * P : (j + 1) * P], col[:, b : b + 1].to_broadcast([P, P]), ident[:])
            return bank

        max_bank = spread(n_max, "max_bank", "turn1")
        n_max_wide = sb.tile([P, n_direct * P], F32, name="n_max_wide")
        nc.scalar.copy(n_max_wide[:], max_bank[:])
        rho_wide = spread(rho, "rho_wide", "rho")
        kl_wide = spread(kl, "kl_wide", "kl")

        sums = [sb.tile([P, GROUPS], F32, name="sums%d" % i) for i in range(PARTS)]
        dev = [sb.tile([P, GROUPS, D], F32, name="dev%d" % i) for i in range(PARTS)]
        sq = [sb.tile([P, GROUPS, D], F32, name="sq%d" % i) for i in range(PARTS)]
        sq_sums = [sb.tile([P, GROUPS], F32, name="sq_sums%d" % i) for i in range(PARTS)]
        inv_sd = [sb.tile([P, GROUPS], F32, name="inv_sd%d" % i) for i in range(PARTS)]
        adv = sb.tile([P, S], F32, name="adv")

        def over_group(t):
            return t[:].unsqueeze(2).to_broadcast([P, GROUPS, D])

        for h in range(2):
            mine = range(h * per_half, (h + 1) * per_half)
            for i in mine:
                nc.vector.tensor_reduce(sums[i][:], y[i][:], AXIS_X, ALU.add)
            for i in mine:
                nc.vector.scalar_tensor_tensor(dev[i][:], over_group(sums[i]), -1.0 / D, y[i][:], ALU.mult, ALU.add)
                nc.scalar.activation(sq[i][:], dev[i][:], ACT.Square)
        for i in range(PARTS):
            nc.vector.tensor_reduce(sq_sums[i][:], sq[i][:], AXIS_X, ALU.add)
            nc.scalar.activation(inv_sd[i][:], sq_sums[i][:], ACT.Abs_reciprocal_sqrt, bias=0.1, scale=1.0 / D)
        for i in range(PARTS):
            nc.vector.tensor_tensor(
                adv[:, i * PART : (i + 1) * PART].rearrange("p (g d) -> p g d", d=D),
                dev[i][:],
                over_group(inv_sd[i]),
                ALU.mult,
            )

        widths = TURNED + DIRECT
        starts = [sum(widths[:c]) for c in range(len(widths))]
        got = [sb.tile([P, n * P], F32, name="got%d" % c) for c, n in enumerate(widths)]
        res = [sb.tile([P, n * P], F32, name="res%d" % c) for c, n in enumerate(widths)]
        turned_chunks = range(len(TURNED))
        direct_chunks = range(len(TURNED), len(widths))

        def offsets(c):
            return ans_sb[:, starts[c] * 8 : (starts[c] + widths[c]) * 8]

        def tokens(c):
            return slice(starts[c] * P, (starts[c] + widths[c]) * P)

        def wide_cols(c):
            return slice((starts[c] - first_direct) * P, (starts[c] - first_direct + widths[c]) * P)

        for c in turned_chunks:
            nc.vector.tensor_copy(got[c][:], adv[:].indirect(offsets(c)))
        for c in direct_chunks:
            nc.vector.tensor_tensor(got[c][:], adv[:].indirect(offsets(c)), n_max_wide[:, wide_cols(c)], ALU.mult)

        back = []
        for c in turned_chunks:
            n = widths[c]
            turned = ps.tile([P, n, P], F32, name="turned%d" % c, tag=["turn0", "turn1", "wide3"][c])
            for j in range(n):
                nc.tensor.transpose(turned[:, j, :], got[c][:, j * P : (j + 1) * P], ident[:])
            bent = sb.tile([P, n, P], F32, name="bent%d" % c)
            line = sb.tile([P, n, P], F32, name="line%d" % c)
            bank = ps.tile([P, n * P], F32, name="back%d" % c, tag=["wide0", "wide1", "wide2"][c])
            for j in range(n):
                b = starts[c] + j
                nc.scalar.activation(bent[:, j, :], turned[:, j, :], ACT.Relu, scale=n_gap[:, b : b + 1])
                nc.scalar.activation(
                    line[:, j, :], turned[:, j, :], ACT.Identity, scale=n_min[:, b : b + 1], bias=kl[:, b : b + 1]
                )
                cols_j = bank[:, j * P : (j + 1) * P]
                nc.tensor.matmul(cols_j, bent[:, j, :], ident[:], start=True, stop=False, is_transpose=True)
                nc.tensor.matmul(cols_j, line[:, j, :], ident[:], start=False, stop=True, is_transpose=True)
            back.append(bank)

        low = {c: sb.tile([P, widths[c] * P], F32, name="low%d" % c) for c in direct_chunks}
        high = {c: sb.tile([P, widths[c] * P], F32, name="high%d" % c) for c in direct_chunks}
        for c in direct_chunks:
            nc.vector.scalar_tensor_tensor(low[c][:], got[c][:], 0.0, rho_wide[:, wide_cols(c)], ALU.min, ALU.mult)
            nc.vector.scalar_tensor_tensor(high[c][:], got[c][:], 0.0, kl_wide[:, wide_cols(c)], ALU.max, ALU.add)
        for c in turned_chunks:
            nc.scalar.activation(res[c][:], back[c][:], ACT.Copy, scale=-1.0)
            queue = nc.scalar if c == turned_chunks[-1] else nc.sync
            queue.dma_start(out[:, tokens(c)], res[c][:])
        for c in direct_chunks:
            nc.vector.scalar_tensor_tensor(res[c][:], low[c][:], -1.0, high[c][:], ALU.mult, ALU.subtract)
            nc.sync.dma_start(out[:, tokens(c)], res[c][:])
